import numpy as np
import ml_dtypes


def mxq(x, axis, fmt="e4m3"):
    dtype, down = {"e4m3": (ml_dtypes.float8_e4m3fn, 7), "e5m2": (ml_dtypes.float8_e5m2, 14)}[fmt]
    v = np.moveaxis(np.asarray(x, np.float32).astype(ml_dtypes.bfloat16).astype(np.float64), axis, -1)
    blocks = v.reshape(v.shape[:-1] + (-1, 32))
    amax = np.abs(blocks).max(-1, keepdims=True)
    byte = np.maximum(np.where(amax > 0, np.frexp(amax)[1] - 1 + 127, 0) - down, 1)
    scale = np.exp2(byte - 127.0)
    codes = (blocks / scale).astype(np.float32).astype(dtype).astype(np.float64)
    return np.moveaxis((codes * scale).reshape(v.shape), -1, axis)


WIDE = False


def mx_kscale(k):
    if not WIDE:
        return np.ones(k)
    levels = np.array([10, -10, 5, -5, 0])
    if k % 512:
        return np.exp2(np.random.permutation(np.resize(levels, k // 32))).repeat(32)
    a = np.empty((k // 512, 16))
    for p in range(k // 512):
        a[p, :8] = np.random.permutation(np.resize(levels, 8))
        for g in range(8):
            far = levels[np.abs(levels - a[p, g]) >= 10]
            a[p, g + 8] = far[np.random.randint(len(far))]
    return np.exp2(a.ravel()).repeat(32)


def f64(x):
    return np.asarray(x).astype(np.float64)


def striped(idx):
    return np.tile(np.asarray(idx).reshape(-1, 16).T, (8, 1)).astype(np.uint16)


def unstriped(offs):
    return offs[:16].T.reshape(-1).astype(np.int64)


def striped8(idx):
    return np.asarray(idx).reshape(8, -1, 16).transpose(0, 2, 1).reshape(128, -1).astype(np.uint16)


def unstriped8(offs):
    return offs.reshape(8, 16, -1).transpose(0, 2, 1).reshape(8, -1).astype(np.int64)


def pick8(x, idx, run):
    r = np.arange(len(x))
    return x[r[:, None], idx[r % (8 * run) // run]]


E2M1 = np.array([0.0, 0.5, 1.0, 1.5, 2.0, 3.0, 4.0, 6.0, -0.0, -0.5, -1.0, -1.5, -2.0, -3.0, -4.0, -6.0])


def pack_weight(w, fmt):
    k, n = w.shape
    w = f64(np.asarray(w, np.float32).astype(ml_dtypes.bfloat16)).reshape(k // 32, 32, n)
    amax = np.abs(w).max(1)
    if fmt == "e4m3":
        byte = np.frexp(amax)[1] - 1 + 127 - 7
    else:
        mant, ex = np.frexp(amax / 6.0)
        byte = np.where(mant > 0.5, ex, ex - 1) + 127
    byte = np.clip(np.where(amax > 0, byte, 1), 1, 254)
    scaled = (w * np.exp2(127.0 - byte)[:, None, :]).reshape(k, n).astype(np.float32)
    by_word = np.ascontiguousarray(scaled.reshape(k // 512, 128, 4, n).transpose(0, 1, 3, 2))
    if fmt == "e4m3":
        words = by_word.astype(ml_dtypes.float8_e4m3fn).view(np.uint8)
    else:
        c = by_word.astype(ml_dtypes.float4_e2m1fn).view(np.uint8) & 0xF
        words = (c[..., 0::2] | (c[..., 1::2] << 4)).reshape(k // 512, 128, 2 * n)
    return np.ascontiguousarray(words), np.ascontiguousarray(byte.astype(np.uint8).reshape(k // 512, 16, n))


def unpack_weight(words, scales, fmt):
    g, _, n = scales.shape
    words = np.ascontiguousarray(words).reshape(g, 128, n, -1)
    if fmt == "e4m3":
        vals = words.view(ml_dtypes.float8_e4m3fn).astype(np.float64)
    else:
        nib = np.empty((g, 128, n, 4), np.uint8)
        nib[..., 0::2] = words & 0xF
        nib[..., 1::2] = words >> 4
        vals = E2M1[nib]
    vals = vals * np.repeat(np.exp2(scales.astype(np.float64) - 127.0), 8, axis=1)[..., None]
    return vals.transpose(0, 1, 3, 2).reshape(g * 512, n)


K, R, F, T, J, U = 512, 256, 512, 2048, 512, 1024


def setup_inputs():
    n = np.random.standard_normal
    idx = np.random.permutation(T)[:J]
    idx2 = np.stack([np.random.permutation(U)[:J] for _ in range(8)])
    fk = mx_kscale(K)
    ff = mx_kscale(F)
    tabp = pack_weight(n((K, T)) / fk[:, None], "e4m3")
    return {
        "tab_words": tabp[0],
        "tab_scales": tabp[1],
        "w1": (n((K, R)) * 1 / np.sqrt(K) * fk[:, None]).astype(np.float32),
        "gain": (np.random.uniform(0.5, 1.5, (R, 1))).astype(np.float32),
        "ground": (n((R, U)) * 0.7).astype(np.float32),
        "wo": (n((F, R)) * 1 / np.sqrt(F) * ff[:, None]).astype(np.float32),
        "dy": (n((F, U)) / ff[:, None]).astype(np.float32),
        "old": (0.5 * n((R, J))).astype(np.float32),
        "offs": striped(idx),
        "offs2": striped8(idx2),
    }


def reference(tab_words, tab_scales, w1, gain, ground, wo, dy, old, offs, offs2):
    idx = unstriped(offs)
    idx2 = unstriped8(offs2)
    tabu = unpack_weight(tab_words, tab_scales, "e4m3")
    w1q = mxq(f64(w1), 0, "e4m3")
    tabidxg = tabu[:, idx]
    a = w1q.T @ tabidxg
    h1 = a * f64(gain)
    pg = np.zeros((R, U))
    pg[np.arange(R)[:, None], idx2[np.arange(R) % 128 // 16]] = h1
    s = pg + f64(ground)
    u1 = np.tanh(s)
    woq = mxq(f64(wo), 0, "e4m3")
    dyq = mxq(f64(dy), 0, "e4m3")
    c0 = woq.T @ dyq
    ds = c0 * (1.0 - np.square(u1))
    dh1 = pick8(ds, idx2, 16)
    da = dh1 * f64(gain)
    y = da + f64(old)
    return y

@@ -1,0 +1,236 @@
+from contextlib import ExitStack
+
+import concourse.mybir as mybir
+from concourse.masks import make_identity
+
+K, R, F, T, J, U = 512, 256, 512, 2048, 512, 1024
+FLOPS = 2 * K * R * J + 2 * F * R * U
+
+F32 = mybir.dt.float32
+BF16 = mybir.dt.bfloat16
+I32 = mybir.dt.int32
+U32 = mybir.dt.uint32
+U16 = mybir.dt.uint16
+U8 = mybir.dt.uint8
+FP8X4 = mybir.dt.float8_e4m3fn_x4
+ACT = mybir.ActivationFunctionType
+ALU = mybir.AluOpType
+
+P = 128
+PACK = 4
+BANK = 512
+HALVES = R // P
+LIST_COLS = J // 16
+
+
+def weave_views(dst, src):
+    return (
+        dst.rearrange("p (c i) t -> p c t i", i=4),
+        src.rearrange("p t (c i) -> p c t i", i=4),
+    )
+
+
+def tile_attend_cpageput_kernel(tc, tab_words, tab_scales, w1, gain, ground, wo, dy, old, offs, offs2, out):
+    nc = tc.nc
+    with ExitStack() as ctx:
+        keep = ctx.enter_context(tc.tile_pool(name="keep", bufs=1))
+        psum = ctx.enter_context(tc.psum_pool(name="psum", bufs=1))
+
+        def sb(name, shape, dtype, tag=None):
+            return keep.tile(shape, dtype, name=name, tag=tag or name, align_bytes=64)
+
+        def bank(tag, name):
+            return psum.tile([P, BANK], F32, name=name, tag=tag)
+
+        cols = keep.tile([P, LIST_COLS], U16, name="cols")
+        places = keep.tile([P, LIST_COLS], U16, name="places")
+        words = sb("words", [P, T], U32)
+        scale_bytes = sb("scale_bytes", [P, T], U8)
+        gains = sb("gains", [P, HALVES], F32)
+        w1_raw = [sb(f"w1_raw{h}", [P, PACK, P], F32) for h in range(HALVES)]
+        wo_raw = sb("wo_raw", [P, PACK, R], F32)
+        dy_raw = [sb(f"dy_raw{b}", [P, PACK, BANK], F32) for b in range(2)]
+        ground_sb = [sb(f"ground{h}", [P, U], F32) for h in range(HALVES)]
+        old_sb = sb("old_sb", [P, HALVES, J], F32)
+        page = [sb(f"page{h}", [P, U], F32) for h in range(HALVES)]
+        ident = sb("ident", [P, P], F32)
+
+        nc.vector.memset(scale_bytes[:].bitcast(I32), 0)
+        w1_rows = w1.rearrange("(p t) r -> p t r", t=PACK)
+        dy_rows = dy.rearrange("(p t) u -> p t u", t=PACK)
+        nc.sync.dma_start(cols[:], offs)
+        nc.sync.dma_start(w1_raw[0][:], w1_rows[:, :, 0:P])
+        for q in range(4):
+            nc.sync.dma_start(
+                scale_bytes[32 * q : 32 * q + 4, :].bitcast(I32), tab_scales[0, 4 * q : 4 * q + 4, :].bitcast(I32)
+            )
+        nc.sync.dma_start(words[:].bitcast(I32), tab_words[0].rearrange("p n t -> p (n t)").bitcast(I32))
+        nc.sync.dma_start(w1_raw[1][:], w1_rows[:, :, P : 2 * P])
+        nc.sync.dma_start(places[:], offs2)
+        with nc.allow_non_contiguous_dma(reason="one gain to a partition"):
+            nc.sync.dma_start(gains[:], gain.rearrange("(h p) o -> p (h o)", p=P))
+        nc.sync.dma_start(wo_raw[:], wo.rearrange("(p t) r -> p t r", t=PACK))
+        for b in range(2):
+            nc.sync.dma_start(dy_raw[b][:], dy_rows[:, :, b * BANK : (b + 1) * BANK])
+            nc.sync.dma_start(ground_sb[b][:], ground[b * P : (b + 1) * P, :])
+        nc.sync.dma_start(old_sb[:], old.rearrange("(h p) j -> p h j", p=P))
+
+        nc.vector.memset(page[0][:], 0.0)
+        make_identity(nc, ident[:])
+        nc.gpsimd.memset(page[1][:], 0.0)
+
+        got_words = sb("got_words", [P, J], U32)
+        got_bytes = sb("got_bytes", [P, J], U8)
+        w1_bf = sb("w1_bf", [P, R, PACK], BF16)
+        w1_codes = sb("w1_codes", [P, R], U32)
+        w1_scales = sb("w1_scales", [P, R], U8)
+        def quantise_w1(h):
+            r = slice(h * P, (h + 1) * P)
+            d, s = weave_views(w1_bf[:, r, :], w1_raw[h][:])
+            if h == 0:
+                nc.scalar.activation(d, s, ACT.Copy)
+            else:
+                nc.vector.tensor_copy(d, s)
+            nc.vector.quantize_mx(
+                w1_codes[:, r].bitcast(FP8X4), w1_scales[:, r], w1_bf[:, r, :].rearrange("p r t -> p (r t)")
+            )
+
+        quantise_w1(0)
+
+        HJ = J // 2
+        HC = LIST_COLS // 2
+
+        def first_layer(h, piece, acc):
+            nc.tensor.matmul_mx(
+                acc,
+                lhsT=w1_codes[:, h * P : (h + 1) * P].bitcast(FP8X4),
+                lhsT_scale=w1_scales[:, h * P : (h + 1) * P],
+                rhs=got_words[:, piece * HJ : (piece + 1) * HJ].bitcast(FP8X4),
+                rhs_scale=got_bytes[:, piece * HJ : (piece + 1) * HJ],
+                start=True,
+                stop=True,
+            )
+
+        def put(h, piece, acc, tag):
+            h1 = sb(f"h1_{h}{piece}", [P, HJ], F32, tag=tag)
+            nc.scalar.activation(h1[:], acc, ACT.Copy, scale=gains[:, h : h + 1])
+
+            nc.vector.tensor_copy(page[h][:].indirect(places[:, piece * HC : (piece + 1) * HC]), h1[:])
+
+        a0 = [bank(f"back0{piece}", f"a0_{piece}") for piece in range(2)]
+        a1 = [bank(f"turned1{piece}", f"a1_{piece}") for piece in range(2)]
+        for piece in range(2):
+            nc.vector.tensor_copy(
+                got_words[:, piece * HJ : (piece + 1) * HJ], words[:].indirect(cols[:, piece * HC : (piece + 1) * HC])
+            )
+            nc.vector.tensor_copy(
+                got_bytes[:, piece * HJ : (piece + 1) * HJ],
+                scale_bytes[:].indirect(cols[:, piece * HC : (piece + 1) * HC]),
+            )
+            first_layer(0, piece, a0[piece][:, 0:HJ])
+        quantise_w1(1)
+        for piece in range(2):
+            first_layer(1, piece, a1[piece][:, 0:HJ])
+
+        wo_bf = sb("wo_bf", [P, R, PACK], BF16)
+        wo_codes = sb("wo_codes", [P, R], U32)
+        wo_scales = sb("wo_scales", [P, R], U8)
+        dy_bf = [sb(f"dy_bf{b}", [P, BANK, PACK], BF16) for b in range(2)]
+        dy_codes = [sb(f"dy_codes{b}", [P, BANK], U32) for b in range(2)]
+        dy_scales = [sb(f"dy_scales{b}", [P, BANK], U8) for b in range(2)]
+        c0n = {}
+
+        def quantise_dy(b):
+            d, s = weave_views(dy_bf[b][:], dy_raw[b][:])
+            nc.scalar.activation(d, s, ACT.Copy)
+            nc.vector.quantize_mx(
+                dy_codes[b][:].bitcast(FP8X4), dy_scales[b][:], dy_bf[b][:].rearrange("p u t -> p (u t)")
+            )
+
+        def last_layer(h, bs):
+            for b in bs:
+                c0n[h, b] = bank(f"turned{h}{1 - b}", f"c{h}{b}")
+                nc.tensor.matmul_mx(
+                    c0n[h, b][:],
+                    lhsT=wo_codes[:, h * P : (h + 1) * P].bitcast(FP8X4),
+                    lhsT_scale=wo_scales[:, h * P : (h + 1) * P],
+                    rhs=dy_codes[b][:].bitcast(FP8X4),
+                    rhs_scale=dy_scales[b][:],
+                    start=True,
+                    stop=True,
+                )
+
+        ds = [sb(f"ds{h}", [P, U], F32) for h in range(HALVES)]
+        uT = {}
+
+        def turned_tanh(h):
+            turned = [bank(f"turned{h}{b}", f"sT{h}{b}") for b in range(2)]
+            for source, first in ((ground_sb[h], True), (page[h], False)):
+                for b in range(2):
+                    for k in range(4):
+                        nc.tensor.matmul(
+                            turned[b][:, k * P : (k + 1) * P],
+                            source[:, b * BANK + k * P : b * BANK + (k + 1) * P],
+                            ident[:],
+                            start=(first and k == 0),
+                            stop=(not first and k == 3),
+                            is_transpose=True,
+                        )
+            for b in range(2):
+                uT[h, b] = sb(f"uT{h}{b}", [P, BANK], F32)
+                nc.scalar.activation(uT[h, b][:], turned[b][:], ACT.Tanh)
+
+        u2 = {}
+
+        def square(h):
+            if h == 0:
+                both = sb("u20", [P, U], F32, tag="dy_raw1")
+            for b in range(2):
+                u2[h, b] = both[:, b * BANK : (b + 1) * BANK] if h == 0 else sb(f"u2{h}{b}", [P, BANK], F32)[:]
+                back = bank(f"back{h}{b}", f"u{h}{b}")
+                for k in range(4):
+                    nc.tensor.transpose(back[:, k * P : (k + 1) * P], uT[h, b][:, k * P : (k + 1) * P], ident[:])
+                nc.scalar.activation(u2[h, b], back[:], ACT.Square)
+
+        def slope(h):
+            for b in range(2):
+                nc.vector.scalar_tensor_tensor(
+                    ds[h][:, b * BANK : (b + 1) * BANK], u2[h, b], 1.0, c0n[h, b][:], ALU.subtract, ALU.mult
+                )
+
+        def finish(h, pieces):
+            picked = sb(f"picked{h}", [P, J], F32)
+            result = sb(f"result{h}", [P, J], F32, tag="u210" if h == 0 else None)
+            n = J // pieces
+            for piece in range(pieces):
+                nc.vector.tensor_copy(
+                    picked[:, piece * n : (piece + 1) * n],
+                    ds[h][:].indirect(places[:, piece * n // 16 : (piece + 1) * n // 16]),
+                )
+            for piece in range(pieces):
+                c = slice(piece * n, (piece + 1) * n)
+                nc.vector.scalar_tensor_tensor(
+                    result[:, c], picked[:, c], gains[:, h : h + 1], old_sb[:, h, c], ALU.mult, ALU.add
+                )
+                nc.sync.dma_start(out[h * P : (h + 1) * P, c], result[:, c])
+
+
+        put(0, 0, a0[0][:, 0:HJ], None)
+        put(0, 1, a0[1][:, 0:HJ], None)
+        put(1, 0, a1[0][:, 0:HJ], None)
+        d, s = weave_views(wo_bf[:], wo_raw[:])
+        nc.scalar.activation(d, s, ACT.Copy, scale=-1.0)
+        nc.vector.quantize_mx(wo_codes[:].bitcast(FP8X4), wo_scales[:], wo_bf[:].rearrange("p r t -> p (r t)"))
+        quantise_dy(0)
+        put(1, 1, a1[1][:, 0:HJ], "dy_raw0")
+        turned_tanh(0)
+        quantise_dy(1)
+        square(0)
+        last_layer(0, [0, 1])
+        slope(0)
+        turned_tanh(1)
+        square(1)
+        last_layer(1, [0, 1])
+        slope(1)
+        finish(0, 1)
+        finish(1, 2)

@@ -47,15 +47,19 @@ def tile_attend_cpageput_kernel(tc, tab_words, tab_scales, w1, gain, ground, wo,
         words = sb("words", [P, T], U32)
         scale_bytes = sb("scale_bytes", [P, T], U8)
         gains = sb("gains", [P, HALVES], F32)
+        gain_rows = sb("gain_rows", [P, P], F32)
         w1_raw = [sb(f"w1_raw{h}", [P, PACK, P], F32) for h in range(HALVES)]
         wo_raw = sb("wo_raw", [P, PACK, R], F32)
-        dy_raw = [sb(f"dy_raw{b}", [P, PACK, BANK], F32) for b in range(2)]
-        ground_sb = [sb(f"ground{h}", [P, U], F32) for h in range(HALVES)]
+        dy_raw = [sb("dy_raw0", [P, PACK, BANK], F32)]
+        dy_late = [sb(f"dy_late{i}", [P, PACK, BANK // 2], F32) for i in range(2)]
+        ground_sb = [sb("ground0", [P, U], F32)]
+        ground_late = [sb(f"ground_late{i}", [P, BANK], F32) for i in range(2)]
         old_sb = sb("old_sb", [P, HALVES, J], F32)
         page = [sb(f"page{h}", [P, U], F32) for h in range(HALVES)]
         ident = sb("ident", [P, P], F32)
 
         nc.vector.memset(scale_bytes[:].bitcast(I32), 0)
+        nc.vector.memset(gain_rows[:], 0.0)
         w1_rows = w1.rearrange("(p t) r -> p t r", t=PACK)
         dy_rows = dy.rearrange("(p t) u -> p t u", t=PACK)
         nc.sync.dma_start(cols[:], offs)
@@ -64,30 +68,36 @@ def tile_attend_cpageput_kernel(tc, tab_words, tab_scales, w1, gain, ground, wo,
             nc.sync.dma_start(
                 scale_bytes[32 * q : 32 * q + 4, :].bitcast(I32), tab_scales[0, 4 * q : 4 * q + 4, :].bitcast(I32)
             )
+        nc.sync.dma_start(gain_rows[0:HALVES, :], gain.rearrange("(h p) o -> h (p o)", p=P))
         nc.sync.dma_start(words[:].bitcast(I32), tab_words[0].rearrange("p n t -> p (n t)").bitcast(I32))
-        nc.sync.dma_start(w1_raw[1][:], w1_rows[:, :, P : 2 * P])
+        nc.sync.dma_start(w1_raw[1][:], w1_rows[:, :, P:R])
         nc.sync.dma_start(places[:], offs2)
-        with nc.allow_non_contiguous_dma(reason="one gain to a partition"):
-            nc.sync.dma_start(gains[:], gain.rearrange("(h p) o -> p (h o)", p=P))
         nc.sync.dma_start(wo_raw[:], wo.rearrange("(p t) r -> p t r", t=PACK))
-        for b in range(2):
-            nc.sync.dma_start(dy_raw[b][:], dy_rows[:, :, b * BANK : (b + 1) * BANK])
-            nc.sync.dma_start(ground_sb[b][:], ground[b * P : (b + 1) * P, :])
+        nc.sync.dma_start(dy_raw[0][:], dy_rows[:, :, 0:BANK])
+        nc.sync.dma_start(ground_sb[0][:], ground[0:P, :])
+        nc.sync.dma_start(dy_late[1][:], dy_rows[:, :, BANK + 256 : U])
+        nc.sync.dma_start(dy_late[0][:], dy_rows[:, :, BANK : BANK + 256])
+        nc.sync.dma_start(ground_late[0][:], ground[P:R, 0:BANK])
+        nc.sync.dma_start(ground_late[1][:], ground[P:R, BANK:U])
         nc.sync.dma_start(old_sb[:], old.rearrange("(h p) j -> p h j", p=P))
 
-        nc.vector.memset(page[0][:], 0.0)
+        for h in range(HALVES):
+            nc.vector.memset(page[h][:], 0.0)
         make_identity(nc, ident[:])
-        nc.gpsimd.memset(page[1][:], 0.0)
+        gain_bank = bank("x0", "gain_bank")
+        nc.tensor.transpose(gain_bank[:, 0:P], gain_rows[:], ident[:])
+        nc.scalar.copy(gains[:], gain_bank[:, 0:HALVES])
 
         got_words = sb("got_words", [P, J], U32)
         got_bytes = sb("got_bytes", [P, J], U8)
         w1_bf = sb("w1_bf", [P, R, PACK], BF16)
         w1_codes = sb("w1_codes", [P, R], U32)
         w1_scales = sb("w1_scales", [P, R], U8)
-        def quantise_w1(h):
-            r = slice(h * P, (h + 1) * P)
-            d, s = weave_views(w1_bf[:, r, :], w1_raw[h][:])
-            if h == 0:
+        nc.vector.tensor_copy(got_bytes[:], scale_bytes[:].indirect(cols[:]))
+
+        def quantise_w1(r, raw, on_scalar):
+            d, s = weave_views(w1_bf[:, r, :], raw)
+            if on_scalar:
                 nc.scalar.activation(d, s, ACT.Copy)
             else:
                 nc.vector.tensor_copy(d, s)
@@ -95,7 +105,7 @@ def tile_attend_cpageput_kernel(tc, tab_words, tab_scales, w1, gain, ground, wo,
                 w1_codes[:, r].bitcast(FP8X4), w1_scales[:, r], w1_bf[:, r, :].rearrange("p r t -> p (r t)")
             )
 
-        quantise_w1(0)
+        quantise_w1(slice(0, P), w1_raw[0][:], True)
 
         HJ = J // 2
         HC = LIST_COLS // 2
@@ -111,24 +121,21 @@ def tile_attend_cpageput_kernel(tc, tab_words, tab_scales, w1, gain, ground, wo,
                 stop=True,
             )
 
-        def put(h, piece, acc, tag):
-            h1 = sb(f"h1_{h}{piece}", [P, HJ], F32, tag=tag)
-            nc.scalar.activation(h1[:], acc, ACT.Copy, scale=gains[:, h : h + 1])
+        a0 = [bank(f"a{piece}", f"a0_{piece}") for piece in range(2)]
+        a1 = [bank(["t10","t11"][piece], f"a1_{piece}") for piece in range(2)]
+        acc = [a0, a1]
 
+        def put(h, piece, tag):
+            h1 = sb(f"h1_{h}{piece}", [P, HJ], F32, tag=tag)
+            nc.scalar.activation(h1[:], acc[h][piece][:, 0:HJ], ACT.Copy, scale=gains[:, h : h + 1])
             nc.vector.tensor_copy(page[h][:].indirect(places[:, piece * HC : (piece + 1) * HC]), h1[:])
 
-        a0 = [bank(f"back0{piece}", f"a0_{piece}") for piece in range(2)]
-        a1 = [bank(f"turned1{piece}", f"a1_{piece}") for piece in range(2)]
         for piece in range(2):
             nc.vector.tensor_copy(
                 got_words[:, piece * HJ : (piece + 1) * HJ], words[:].indirect(cols[:, piece * HC : (piece + 1) * HC])
             )
-            nc.vector.tensor_copy(
-                got_bytes[:, piece * HJ : (piece + 1) * HJ],
-                scale_bytes[:].indirect(cols[:, piece * HC : (piece + 1) * HC]),
-            )
             first_layer(0, piece, a0[piece][:, 0:HJ])
-        quantise_w1(1)
+        quantise_w1(slice(P, R), w1_raw[1][:], False)
         for piece in range(2):
             first_layer(1, piece, a1[piece][:, 0:HJ])
 
@@ -140,33 +147,52 @@ def tile_attend_cpageput_kernel(tc, tab_words, tab_scales, w1, gain, ground, wo,
         dy_scales = [sb(f"dy_scales{b}", [P, BANK], U8) for b in range(2)]
         c0n = {}
 
-        def quantise_dy(b):
-            d, s = weave_views(dy_bf[b][:], dy_raw[b][:])
-            nc.scalar.activation(d, s, ACT.Copy)
-            nc.vector.quantize_mx(
-                dy_codes[b][:].bitcast(FP8X4), dy_scales[b][:], dy_bf[b][:].rearrange("p u t -> p (u t)")
-            )
+        def quantise_wo():
+            d, s = weave_views(wo_bf[:], wo_raw[:])
+            nc.scalar.activation(d, s, ACT.Copy, scale=-1.0)
+            nc.vector.quantize_mx(wo_codes[:].bitcast(FP8X4), wo_scales[:], wo_bf[:].rearrange("p r t -> p (r t)"))
 
-        def last_layer(h, bs):
-            for b in bs:
-                c0n[h, b] = bank(f"turned{h}{1 - b}", f"c{h}{b}")
+        def quantise_dy(b, pieces):
+            n = BANK // pieces
+            for piece in range(pieces):
+                c = slice(piece * n, (piece + 1) * n)
+                d, s = weave_views(dy_bf[b][:, c, :], dy_raw[0][:] if b == 0 else dy_late[piece][:])
+                if (b, piece) == (1, 0):
+                    nc.vector.tensor_copy(d, s)
+                else:
+                    nc.scalar.activation(d, s, ACT.Copy)
+                nc.vector.quantize_mx(
+                    dy_codes[b][:, c].bitcast(FP8X4), dy_scales[b][:, c], dy_bf[b][:, c, :].rearrange("p u t -> p (u t)")
+                )
+
+        def last_layer(h, b, pieces):
+            c0n[h, b] = bank({"10":"x0","11":"x1","00":"t01","01":"t00"}[f"{h}{b}"], f"c{h}{b}")
+            n = BANK // pieces
+            for piece in range(pieces):
+                c = slice(piece * n, (piece + 1) * n)
                 nc.tensor.matmul_mx(
-                    c0n[h, b][:],
+                    c0n[h, b][:, c],
                     lhsT=wo_codes[:, h * P : (h + 1) * P].bitcast(FP8X4),
                     lhsT_scale=wo_scales[:, h * P : (h + 1) * P],
-                    rhs=dy_codes[b][:].bitcast(FP8X4),
-                    rhs_scale=dy_scales[b][:],
+                    rhs=dy_codes[b][:, c].bitcast(FP8X4),
+                    rhs_scale=dy_scales[b][:, c],
                     start=True,
                     stop=True,
                 )
 
         ds = [sb(f"ds{h}", [P, U], F32) for h in range(HALVES)]
         uT = {}
+        u2 = {}
+        ADD = ["PE","V"]
 
-        def turned_tanh(h):
-            turned = [bank(f"turned{h}{b}", f"sT{h}{b}") for b in range(2)]
-            for source, first in ((ground_sb[h], True), (page[h], False)):
-                for b in range(2):
+        def tanh(h):
+            if ADD[h] == "PE":
+                turned = [bank(f"t{h}{b}", f"sT{h}{b}") for b in range(2)]
+                steps = [(b, first) for first in (True, False) for b in range(2)]
+                if "gg"[h] == "b":
+                    steps = [(b, first) for b in range(2) for first in (True, False)]
+                for b, first in steps:
+                    source = ground_sb[h] if first else page[h]
                     for k in range(4):
                         nc.tensor.matmul(
                             turned[b][:, k * P : (k + 1) * P],
@@ -176,20 +202,29 @@ def tile_attend_cpageput_kernel(tc, tab_words, tab_scales, w1, gain, ground, wo,
                             stop=(not first and k == 3),
                             is_transpose=True,
                         )
+                total = [turned[b][:] for b in range(2)]
+            else:
+                summed = sb(f"s{h}", [P, U], F32)
+                total = [summed[:, b * BANK : (b + 1) * BANK] for b in range(2)]
+                eng = nc.vector if ADD[h] == "V" else nc.gpsimd
+                for b in range(2):
+                    c = slice(b * BANK, (b + 1) * BANK)
+                    eng.tensor_tensor(total[b], page[h][:, c], ground_late[b][:], ALU.add)
             for b in range(2):
                 uT[h, b] = sb(f"uT{h}{b}", [P, BANK], F32)
-                nc.scalar.activation(uT[h, b][:], turned[b][:], ACT.Tanh)
-
-        u2 = {}
+                nc.scalar.activation(uT[h, b][:], total[b], ACT.Tanh)
 
         def square(h):
             if h == 0:
-                both = sb("u20", [P, U], F32, tag="dy_raw1")
+                both = sb("u20", [P, U], F32, tag=None)
             for b in range(2):
                 u2[h, b] = both[:, b * BANK : (b + 1) * BANK] if h == 0 else sb(f"u2{h}{b}", [P, BANK], F32)[:]
-                back = bank(f"back{h}{b}", f"u{h}{b}")
-                for k in range(4):
-                    nc.tensor.transpose(back[:, k * P : (k + 1) * P], uT[h, b][:, k * P : (k + 1) * P], ident[:])
+                if ADD[h] == "PE":
+                    back = bank({"10":"a0","11":"a1","00":"a0","01":"a1"}[f"{h}{b}"], f"u{h}{b}")
+                    for k in range(4):
+                        nc.tensor.transpose(back[:, k * P : (k + 1) * P], uT[h, b][:, k * P : (k + 1) * P], ident[:])
+                else:
+                    back = uT[h, b]
                 nc.scalar.activation(u2[h, b], back[:], ACT.Square)
 
         def slope(h):
@@ -214,23 +249,22 @@ def tile_attend_cpageput_kernel(tc, tab_words, tab_scales, w1, gain, ground, wo,
                 )
                 nc.sync.dma_start(out[h * P : (h + 1) * P, c], result[:, c])
 
-
-        put(0, 0, a0[0][:, 0:HJ], None)
-        put(0, 1, a0[1][:, 0:HJ], None)
-        put(1, 0, a1[0][:, 0:HJ], None)
-        d, s = weave_views(wo_bf[:], wo_raw[:])
-        nc.scalar.activation(d, s, ACT.Copy, scale=-1.0)
-        nc.vector.quantize_mx(wo_codes[:].bitcast(FP8X4), wo_scales[:], wo_bf[:].rearrange("p r t -> p (r t)"))
-        quantise_dy(0)
-        put(1, 1, a1[1][:, 0:HJ], "dy_raw0")
-        turned_tanh(0)
-        quantise_dy(1)
+        put(0, 0, None)
+        put(0, 1, None)
+        put(1, 0, None)
+        quantise_wo()
+        quantise_dy(0, 1)
+        put(1, 1, "dy_raw0")
+        tanh(0)
+        quantise_dy(1, 2)
         square(0)
-        last_layer(0, [0, 1])
+        last_layer(0, 0, 1)
+        last_layer(0, 1, 2)
+        last_layer(1, 0, 1)
+        last_layer(1, 1, 1)
         slope(0)
-        turned_tanh(1)
+        tanh(1)
         square(1)
-        last_layer(1, [0, 1])
         slope(1)
         finish(0, 1)
         finish(1, 2)

@@ -110,34 +110,32 @@ def tile_attend_cpageput_kernel(tc, tab_words, tab_scales, w1, gain, ground, wo,
         HJ = J // 2
         HC = LIST_COLS // 2
 
-        def first_layer(h, piece, acc):
+        def first_layer(h, c, acc):
             nc.tensor.matmul_mx(
                 acc,
                 lhsT=w1_codes[:, h * P : (h + 1) * P].bitcast(FP8X4),
                 lhsT_scale=w1_scales[:, h * P : (h + 1) * P],
-                rhs=got_words[:, piece * HJ : (piece + 1) * HJ].bitcast(FP8X4),
-                rhs_scale=got_bytes[:, piece * HJ : (piece + 1) * HJ],
+                rhs=got_words[:, c].bitcast(FP8X4),
+                rhs_scale=got_bytes[:, c],
                 start=True,
                 stop=True,
             )
 
         a0 = [bank(f"a{piece}", f"a0_{piece}") for piece in range(2)]
-        a1 = [bank(["t10","t11"][piece], f"a1_{piece}") for piece in range(2)]
-        acc = [a0, a1]
+        a1 = bank("x1", "a1")
 
-        def put(h, piece, tag):
-            h1 = sb(f"h1_{h}{piece}", [P, HJ], F32, tag=tag)
-            nc.scalar.activation(h1[:], acc[h][piece][:, 0:HJ], ACT.Copy, scale=gains[:, h : h + 1])
-            nc.vector.tensor_copy(page[h][:].indirect(places[:, piece * HC : (piece + 1) * HC]), h1[:])
+        def put(h, acc, j0, n):
+            h1 = sb(f"h1_{h}{j0}", [P, n], F32)
+            nc.scalar.activation(h1[:], acc[:, 0:n], ACT.Copy, scale=gains[:, h : h + 1])
+            nc.vector.tensor_copy(page[h][:].indirect(places[:, j0 // 16 : (j0 + n) // 16]), h1[:])
 
         for piece in range(2):
             nc.vector.tensor_copy(
                 got_words[:, piece * HJ : (piece + 1) * HJ], words[:].indirect(cols[:, piece * HC : (piece + 1) * HC])
             )
-            first_layer(0, piece, a0[piece][:, 0:HJ])
+            first_layer(0, slice(piece * HJ, (piece + 1) * HJ), a0[piece][:, 0:HJ])
         quantise_w1(slice(P, R), w1_raw[1][:], False)
-        for piece in range(2):
-            first_layer(1, piece, a1[piece][:, 0:HJ])
+        first_layer(1, slice(0, J), a1[:])
 
         wo_bf = sb("wo_bf", [P, R, PACK], BF16)
         wo_codes = sb("wo_codes", [P, R], U32)
@@ -166,7 +164,7 @@ def tile_attend_cpageput_kernel(tc, tab_words, tab_scales, w1, gain, ground, wo,
                 )
 
         def last_layer(h, b, pieces):
-            c0n[h, b] = bank({"10":"x0","11":"x1","00":"t01","01":"t00"}[f"{h}{b}"], f"c{h}{b}")
+            c0n[h, b] = bank({"10":"a0","11":"a1","00":"t01","01":"t00"}[f"{h}{b}"], f"c{h}{b}")
             n = BANK // pieces
             for piece in range(pieces):
                 c = slice(piece * n, (piece + 1) * n)
@@ -249,12 +247,41 @@ def tile_attend_cpageput_kernel(tc, tab_words, tab_scales, w1, gain, ground, wo,
                 )
                 nc.sync.dma_start(out[h * P : (h + 1) * P, c], result[:, c])
 
-        put(0, 0, None)
-        put(0, 1, None)
-        put(1, 0, None)
+        summed = sb("s1", [P, U], F32)
+
+        def add1(b):
+            c = slice(b * BANK, (b + 1) * BANK)
+            nc.vector.tensor_tensor(summed[:, c], page[1][:, c], ground_late[b][:], ALU.add)
+
+        def act1(b):
+            uT[1, b] = sb(f"uT1{b}", [P, BANK], F32)
+            nc.scalar.activation(uT[1, b][:], summed[:, b * BANK : (b + 1) * BANK], ACT.Tanh)
+            u2[1, b] = sb(f"u21{b}", [P, BANK], F32)[:]
+            nc.scalar.activation(u2[1, b], uT[1, b][:], ACT.Square)
+
+        def mult(h, b):
+            nc.vector.scalar_tensor_tensor(
+                ds[h][:, b * BANK : (b + 1) * BANK], u2[h, b], 1.0, c0n[h, b][:], ALU.subtract, ALU.mult
+            )
+
+        picked = [sb(f"picked{h}", [P, J], F32) for h in range(HALVES)]
+
+        def pick(h, j0, n):
+            nc.vector.tensor_copy(picked[h][:, j0 : j0 + n], ds[h][:].indirect(places[:, j0 // 16 : (j0 + n) // 16]))
+
+        def give(h, j0, n, tag):
+            c = slice(j0, j0 + n)
+            result = sb(f"result{h}{j0}", [P, n], F32, tag=tag)
+            nc.vector.scalar_tensor_tensor(
+                result[:], picked[h][:, c], gains[:, h : h + 1], old_sb[:, h, c], ALU.mult, ALU.add
+            )
+            nc.sync.dma_start(out[h * P : (h + 1) * P, c], result[:])
+
+        put(0, a0[0], 0, HJ)
+        put(0, a0[1], HJ, HJ)
+        put(1, a1, 0, J)
         quantise_wo()
         quantise_dy(0, 1)
-        put(1, 1, "dy_raw0")
         tanh(0)
         quantise_dy(1, 2)
         square(0)
@@ -262,9 +289,17 @@ def tile_attend_cpageput_kernel(tc, tab_words, tab_scales, w1, gain, ground, wo,
         last_layer(0, 1, 2)
         last_layer(1, 0, 1)
         last_layer(1, 1, 1)
-        slope(0)
-        tanh(1)
-        square(1)
-        slope(1)
-        finish(0, 1)
-        finish(1, 2)
+        add1(0)
+        add1(1)
+        act1(0)
+        act1(1)
+        mult(0, 0)
+        mult(0, 1)
+        mult(1, 0)
+        pick(0, 0, J)
+        mult(1, 1)
+        give(0, 0, J, "u210")
+        pick(1, 0, HJ)
+        pick(1, HJ, HJ)
+        give(1, 0, HJ, None)
+        give(1, HJ, HJ, None)

@@ -18,15 +18,18 @@ ALU = mybir.AluOpType
 
 P = 128
 PACK = 4
-BANK = 512
+SIDE = 512
+PER_COL = 16
 HALVES = R // P
-LIST_COLS = J // 16
+SIDES = U // SIDE
+RUN = 4
+PIECE = 256
 
 
-def weave_views(dst, src):
+def interleave_views(dst, src):
     return (
-        dst.rearrange("p (c i) t -> p c t i", i=4),
-        src.rearrange("p t (c i) -> p c t i", i=4),
+        dst.rearrange("p (c i) t -> p c t i", i=RUN),
+        src.rearrange("p t (c i) -> p c t i", i=RUN),
     )
 
 
@@ -40,51 +43,68 @@ def tile_attend_cpageput_kernel(tc, tab_words, tab_scales, w1, gain, ground, wo,
             return keep.tile(shape, dtype, name=name, tag=tag or name, align_bytes=64)
 
         def bank(tag, name):
-            return psum.tile([P, BANK], F32, name=name, tag=tag)
+            return psum.tile([P, SIDE], F32, name=name, tag=tag)
 
-        cols = keep.tile([P, LIST_COLS], U16, name="cols")
-        places = keep.tile([P, LIST_COLS], U16, name="places")
+        def entries(lists, start, count):
+            return lists[:, start // PER_COL : (start + count) // PER_COL]
+
+        def quantise(codes, scales, woven):
+            nc.vector.quantize_mx(codes.bitcast(FP8X4), scales, woven.rearrange("p c t -> p (c t)"))
+
+        def product(acc, h, w_codes, w_scales, x_codes, x_scales):
+            rows = slice(h * P, (h + 1) * P)
+            nc.tensor.matmul_mx(
+                acc,
+                lhsT=w_codes[:, rows].bitcast(FP8X4),
+                lhsT_scale=w_scales[:, rows],
+                rhs=x_codes.bitcast(FP8X4),
+                rhs_scale=x_scales,
+                start=True,
+                stop=True,
+            )
+
+        cols = keep.tile([P, J // PER_COL], U16, name="cols")
+        places = keep.tile([P, J // PER_COL], U16, name="places")
         words = sb("words", [P, T], U32)
         scale_bytes = sb("scale_bytes", [P, T], U8)
         gains = sb("gains", [P, HALVES], F32)
         gain_rows = sb("gain_rows", [P, P], F32)
-        w1_raw = [sb(f"w1_raw{h}", [P, PACK, P], F32) for h in range(HALVES)]
+        w1_raw = sb("w1_raw", [P, PACK, R], F32)
         wo_raw = sb("wo_raw", [P, PACK, R], F32)
-        dy_raw = [sb("dy_raw0", [P, PACK, BANK], F32)]
-        dy_late = [sb(f"dy_late{i}", [P, PACK, BANK // 2], F32) for i in range(2)]
-        ground_sb = [sb("ground0", [P, U], F32)]
-        ground_late = [sb(f"ground_late{i}", [P, BANK], F32) for i in range(2)]
+        dy_side0 = sb("dy_side0", [P, PACK, SIDE], F32)
+        dy_side1 = [sb(f"dy_side1_{i}", [P, PACK, PIECE], F32) for i in range(SIDE // PIECE)]
+        ground0 = sb("ground0", [P, U], F32)
+        ground1 = [sb(f"ground1_{s}", [P, SIDE], F32) for s in range(SIDES)]
         old_sb = sb("old_sb", [P, HALVES, J], F32)
         page = [sb(f"page{h}", [P, U], F32) for h in range(HALVES)]
         ident = sb("ident", [P, P], F32)
 
         nc.vector.memset(scale_bytes[:].bitcast(I32), 0)
         nc.vector.memset(gain_rows[:], 0.0)
-        w1_rows = w1.rearrange("(p t) r -> p t r", t=PACK)
         dy_rows = dy.rearrange("(p t) u -> p t u", t=PACK)
         nc.sync.dma_start(cols[:], offs)
-        nc.sync.dma_start(w1_raw[0][:], w1_rows[:, :, 0:P])
+        nc.sync.dma_start(w1_raw[:], w1.rearrange("(p t) r -> p t r", t=PACK))
         for q in range(4):
             nc.sync.dma_start(
                 scale_bytes[32 * q : 32 * q + 4, :].bitcast(I32), tab_scales[0, 4 * q : 4 * q + 4, :].bitcast(I32)
             )
         nc.sync.dma_start(gain_rows[0:HALVES, :], gain.rearrange("(h p) o -> h (p o)", p=P))
         nc.sync.dma_start(words[:].bitcast(I32), tab_words[0].rearrange("p n t -> p (n t)").bitcast(I32))
-        nc.sync.dma_start(w1_raw[1][:], w1_rows[:, :, P:R])
-        nc.sync.dma_start(places[:], offs2)
         nc.sync.dma_start(wo_raw[:], wo.rearrange("(p t) r -> p t r", t=PACK))
-        nc.sync.dma_start(dy_raw[0][:], dy_rows[:, :, 0:BANK])
-        nc.sync.dma_start(ground_sb[0][:], ground[0:P, :])
-        nc.sync.dma_start(dy_late[1][:], dy_rows[:, :, BANK + 256 : U])
-        nc.sync.dma_start(dy_late[0][:], dy_rows[:, :, BANK : BANK + 256])
-        nc.sync.dma_start(ground_late[0][:], ground[P:R, 0:BANK])
-        nc.sync.dma_start(ground_late[1][:], ground[P:R, BANK:U])
+        nc.sync.dma_start(places[:], offs2)
+        nc.sync.dma_start(dy_side0[:], dy_rows[:, :, 0:SIDE])
+        nc.sync.dma_start(ground0[:], ground[0:P, :])
+        for i, raw in enumerate(dy_side1):
+            nc.sync.dma_start(raw[:], dy_rows[:, :, SIDE + i * PIECE : SIDE + (i + 1) * PIECE])
+        nc.sync.dma_start(ground1[0][:], ground[P:R, 0:SIDE])
         nc.sync.dma_start(old_sb[:], old.rearrange("(h p) j -> p h j", p=P))
+        nc.sync.dma_start(ground1[1][:], ground[P:R, SIDE:U])
 
         for h in range(HALVES):
             nc.vector.memset(page[h][:], 0.0)
         make_identity(nc, ident[:])
-        gain_bank = bank("x0", "gain_bank")
+
+        gain_bank = bank("gain", "gain_bank")
         nc.tensor.transpose(gain_bank[:, 0:P], gain_rows[:], ident[:])
         nc.scalar.copy(gains[:], gain_bank[:, 0:HALVES])
 
@@ -95,211 +115,118 @@ def tile_attend_cpageput_kernel(tc, tab_words, tab_scales, w1, gain, ground, wo,
         w1_scales = sb("w1_scales", [P, R], U8)
         nc.vector.tensor_copy(got_bytes[:], scale_bytes[:].indirect(cols[:]))
 
-        def quantise_w1(r, raw, on_scalar):
-            d, s = weave_views(w1_bf[:, r, :], raw)
-            if on_scalar:
-                nc.scalar.activation(d, s, ACT.Copy)
-            else:
-                nc.vector.tensor_copy(d, s)
-            nc.vector.quantize_mx(
-                w1_codes[:, r].bitcast(FP8X4), w1_scales[:, r], w1_bf[:, r, :].rearrange("p r t -> p (r t)")
-            )
+        nc.vector.tensor_copy(*interleave_views(w1_bf[:, 0:P, :], w1_raw[:, :, 0:P]))
+        quantise(w1_codes[:, 0:P], w1_scales[:, 0:P], w1_bf[:, 0:P, :])
+        nc.scalar.activation(*interleave_views(w1_bf[:, P:R, :], w1_raw[:, :, P:R]), ACT.Copy)
+        quantise(w1_codes[:, P:R], w1_scales[:, P:R], w1_bf[:, P:R, :])
 
-        quantise_w1(slice(0, P), w1_raw[0][:], True)
+        a0 = [bank(f"upright{i}", f"a0_{i}") for i in range(J // PIECE)]
+        a1 = bank("a1", "a1")
+        for i, acc in enumerate(a0):
+            c = slice(i * PIECE, (i + 1) * PIECE)
+            nc.vector.tensor_copy(got_words[:, c], words[:].indirect(entries(cols, i * PIECE, PIECE)))
+            product(acc[:, 0:PIECE], 0, w1_codes, w1_scales, got_words[:, c], got_bytes[:, c])
+        product(a1[:], 1, w1_codes, w1_scales, got_words[:], got_bytes[:])
 
-        HJ = J // 2
-        HC = LIST_COLS // 2
+        def put(h, acc, start, count):
+            h1 = sb(f"h1_{h}_{start}", [P, count], F32)
+            nc.scalar.activation(h1[:], acc[:, 0:count], ACT.Copy, scale=gains[:, h : h + 1])
+            nc.vector.tensor_copy(page[h][:].indirect(entries(places, start, count)), h1[:])
 
-        def first_layer(h, c, acc):
-            nc.tensor.matmul_mx(
-                acc,
-                lhsT=w1_codes[:, h * P : (h + 1) * P].bitcast(FP8X4),
-                lhsT_scale=w1_scales[:, h * P : (h + 1) * P],
-                rhs=got_words[:, c].bitcast(FP8X4),
-                rhs_scale=got_bytes[:, c],
-                start=True,
-                stop=True,
-            )
-
-        a0 = [bank(f"a{piece}", f"a0_{piece}") for piece in range(2)]
-        a1 = bank("x1", "a1")
-
-        def put(h, acc, j0, n):
-            h1 = sb(f"h1_{h}{j0}", [P, n], F32)
-            nc.scalar.activation(h1[:], acc[:, 0:n], ACT.Copy, scale=gains[:, h : h + 1])
-            nc.vector.tensor_copy(page[h][:].indirect(places[:, j0 // 16 : (j0 + n) // 16]), h1[:])
-
-        for piece in range(2):
-            nc.vector.tensor_copy(
-                got_words[:, piece * HJ : (piece + 1) * HJ], words[:].indirect(cols[:, piece * HC : (piece + 1) * HC])
-            )
-            first_layer(0, slice(piece * HJ, (piece + 1) * HJ), a0[piece][:, 0:HJ])
-        quantise_w1(slice(P, R), w1_raw[1][:], False)
-        first_layer(1, slice(0, J), a1[:])
+        for i, acc in enumerate(a0):
+            put(0, acc, i * PIECE, PIECE)
+        put(1, a1, 0, J)
 
         wo_bf = sb("wo_bf", [P, R, PACK], BF16)
         wo_codes = sb("wo_codes", [P, R], U32)
         wo_scales = sb("wo_scales", [P, R], U8)
-        dy_bf = [sb(f"dy_bf{b}", [P, BANK, PACK], BF16) for b in range(2)]
-        dy_codes = [sb(f"dy_codes{b}", [P, BANK], U32) for b in range(2)]
-        dy_scales = [sb(f"dy_scales{b}", [P, BANK], U8) for b in range(2)]
-        c0n = {}
+        dy_bf = [sb(f"dy_bf{s}", [P, SIDE, PACK], BF16) for s in range(SIDES)]
+        dy_codes = [sb(f"dy_codes{s}", [P, SIDE], U32) for s in range(SIDES)]
+        dy_scales = [sb(f"dy_scales{s}", [P, SIDE], U8) for s in range(SIDES)]
 
-        def quantise_wo():
-            d, s = weave_views(wo_bf[:], wo_raw[:])
-            nc.scalar.activation(d, s, ACT.Copy, scale=-1.0)
-            nc.vector.quantize_mx(wo_codes[:].bitcast(FP8X4), wo_scales[:], wo_bf[:].rearrange("p r t -> p (r t)"))
+        nc.vector.tensor_scalar(*interleave_views(wo_bf[:], wo_raw[:]), -1.0, None, ALU.mult)
+        quantise(wo_codes[:], wo_scales[:], wo_bf[:])
 
-        def quantise_dy(b, pieces):
-            n = BANK // pieces
-            for piece in range(pieces):
-                c = slice(piece * n, (piece + 1) * n)
-                d, s = weave_views(dy_bf[b][:, c, :], dy_raw[0][:] if b == 0 else dy_late[piece][:])
-                if (b, piece) == (1, 0):
-                    nc.vector.tensor_copy(d, s)
-                else:
-                    nc.scalar.activation(d, s, ACT.Copy)
-                nc.vector.quantize_mx(
-                    dy_codes[b][:, c].bitcast(FP8X4), dy_scales[b][:, c], dy_bf[b][:, c, :].rearrange("p u t -> p (u t)")
+        def quantise_dy(s, c, raw):
+            nc.scalar.activation(*interleave_views(dy_bf[s][:, c, :], raw[:]), ACT.Copy)
+            quantise(dy_codes[s][:, c], dy_scales[s][:, c], dy_bf[s][:, c, :])
+
+        quantise_dy(0, slice(0, SIDE), dy_side0)
+
+        turned = [bank(f"turned{s}", f"sum0_{s}") for s in range(SIDES)]
+        blocks = SIDE // P
+        for source, opens in ((ground0, True), (page[0], False)):
+            for s in range(SIDES):
+                for b in range(blocks):
+                    nc.tensor.matmul(
+                        turned[s][:, b * P : (b + 1) * P],
+                        source[:, s * SIDE + b * P : s * SIDE + (b + 1) * P],
+                        ident[:],
+                        start=(opens and b == 0),
+                        stop=(not opens and b == blocks - 1),
+                        is_transpose=True,
+                    )
+        tanh0_turned = [sb(f"tanh0_turned{s}", [P, SIDE], F32) for s in range(SIDES)]
+        for s in range(SIDES):
+            nc.scalar.activation(tanh0_turned[s][:], turned[s][:], ACT.Tanh)
+
+        for i, raw in enumerate(dy_side1):
+            quantise_dy(1, slice(i * PIECE, (i + 1) * PIECE), raw)
+
+        squares0 = sb("squares0", [P, U], F32)
+        squares = {(0, s): squares0[:, s * SIDE : (s + 1) * SIDE] for s in range(SIDES)}
+        for s in range(SIDES):
+            upright = bank(f"upright{s}", f"tanh0_{s}")
+            for b in range(blocks):
+                nc.tensor.transpose(
+                    upright[:, b * P : (b + 1) * P], tanh0_turned[s][:, b * P : (b + 1) * P], ident[:]
                 )
+            nc.scalar.activation(squares[0, s], upright[:], ACT.Square)
 
-        def last_layer(h, b, pieces):
-            c0n[h, b] = bank({"10":"a0","11":"a1","00":"t01","01":"t00"}[f"{h}{b}"], f"c{h}{b}")
-            n = BANK // pieces
-            for piece in range(pieces):
-                c = slice(piece * n, (piece + 1) * n)
-                nc.tensor.matmul_mx(
-                    c0n[h, b][:, c],
-                    lhsT=wo_codes[:, h * P : (h + 1) * P].bitcast(FP8X4),
-                    lhsT_scale=wo_scales[:, h * P : (h + 1) * P],
-                    rhs=dy_codes[b][:, c].bitcast(FP8X4),
-                    rhs_scale=dy_scales[b][:, c],
-                    start=True,
-                    stop=True,
-                )
+        minus_c0 = {}
+        for h in range(HALVES):
+            for s in range(SIDES):
+                minus_c0[h, s] = bank(f"turned{1 - s}" if h == 0 else f"upright{s}", f"minus_c0_{h}{s}")
+                product(minus_c0[h, s][:], h, wo_codes, wo_scales, dy_codes[s][:], dy_scales[s][:])
+
+        sum1 = sb("sum1", [P, U], F32)
+        for s in range(SIDES):
+            c = slice(s * SIDE, (s + 1) * SIDE)
+            nc.vector.tensor_tensor(sum1[:, c], page[1][:, c], ground1[s][:], ALU.add)
+        for s in range(SIDES):
+            tanh1 = sb(f"tanh1_{s}", [P, SIDE], F32)
+            nc.scalar.activation(tanh1[:], sum1[:, s * SIDE : (s + 1) * SIDE], ACT.Tanh)
+            squares[1, s] = sb(f"squares1_{s}", [P, SIDE], F32)[:]
+            nc.scalar.activation(squares[1, s], tanh1[:], ACT.Square)
 
         ds = [sb(f"ds{h}", [P, U], F32) for h in range(HALVES)]
-        uT = {}
-        u2 = {}
-        ADD = ["PE","V"]
-
-        def tanh(h):
-            if ADD[h] == "PE":
-                turned = [bank(f"t{h}{b}", f"sT{h}{b}") for b in range(2)]
-                steps = [(b, first) for first in (True, False) for b in range(2)]
-                if "gg"[h] == "b":
-                    steps = [(b, first) for b in range(2) for first in (True, False)]
-                for b, first in steps:
-                    source = ground_sb[h] if first else page[h]
-                    for k in range(4):
-                        nc.tensor.matmul(
-                            turned[b][:, k * P : (k + 1) * P],
-                            source[:, b * BANK + k * P : b * BANK + (k + 1) * P],
-                            ident[:],
-                            start=(first and k == 0),
-                            stop=(not first and k == 3),
-                            is_transpose=True,
-                        )
-                total = [turned[b][:] for b in range(2)]
-            else:
-                summed = sb(f"s{h}", [P, U], F32)
-                total = [summed[:, b * BANK : (b + 1) * BANK] for b in range(2)]
-                eng = nc.vector if ADD[h] == "V" else nc.gpsimd
-                for b in range(2):
-                    c = slice(b * BANK, (b + 1) * BANK)
-                    eng.tensor_tensor(total[b], page[h][:, c], ground_late[b][:], ALU.add)
-            for b in range(2):
-                uT[h, b] = sb(f"uT{h}{b}", [P, BANK], F32)
-                nc.scalar.activation(uT[h, b][:], total[b], ACT.Tanh)
-
-        def square(h):
-            if h == 0:
-                both = sb("u20", [P, U], F32, tag=None)
-            for b in range(2):
-                u2[h, b] = both[:, b * BANK : (b + 1) * BANK] if h == 0 else sb(f"u2{h}{b}", [P, BANK], F32)[:]
-                if ADD[h] == "PE":
-                    back = bank({"10":"a0","11":"a1","00":"a0","01":"a1"}[f"{h}{b}"], f"u{h}{b}")
-                    for k in range(4):
-                        nc.tensor.transpose(back[:, k * P : (k + 1) * P], uT[h, b][:, k * P : (k + 1) * P], ident[:])
-                else:
-                    back = uT[h, b]
-                nc.scalar.activation(u2[h, b], back[:], ACT.Square)
-
-        def slope(h):
-            for b in range(2):
-                nc.vector.scalar_tensor_tensor(
-                    ds[h][:, b * BANK : (b + 1) * BANK], u2[h, b], 1.0, c0n[h, b][:], ALU.subtract, ALU.mult
-                )
-
-        def finish(h, pieces):
-            picked = sb(f"picked{h}", [P, J], F32)
-            result = sb(f"result{h}", [P, J], F32, tag="u210" if h == 0 else None)
-            n = J // pieces
-            for piece in range(pieces):
-                nc.vector.tensor_copy(
-                    picked[:, piece * n : (piece + 1) * n],
-                    ds[h][:].indirect(places[:, piece * n // 16 : (piece + 1) * n // 16]),
-                )
-            for piece in range(pieces):
-                c = slice(piece * n, (piece + 1) * n)
-                nc.vector.scalar_tensor_tensor(
-                    result[:, c], picked[:, c], gains[:, h : h + 1], old_sb[:, h, c], ALU.mult, ALU.add
-                )
-                nc.sync.dma_start(out[h * P : (h + 1) * P, c], result[:, c])
-
-        summed = sb("s1", [P, U], F32)
-
-        def add1(b):
-            c = slice(b * BANK, (b + 1) * BANK)
-            nc.vector.tensor_tensor(summed[:, c], page[1][:, c], ground_late[b][:], ALU.add)
-
-        def act1(b):
-            uT[1, b] = sb(f"uT1{b}", [P, BANK], F32)
-            nc.scalar.activation(uT[1, b][:], summed[:, b * BANK : (b + 1) * BANK], ACT.Tanh)
-            u2[1, b] = sb(f"u21{b}", [P, BANK], F32)[:]
-            nc.scalar.activation(u2[1, b], uT[1, b][:], ACT.Square)
-
-        def mult(h, b):
-            nc.vector.scalar_tensor_tensor(
-                ds[h][:, b * BANK : (b + 1) * BANK], u2[h, b], 1.0, c0n[h, b][:], ALU.subtract, ALU.mult
-            )
-
         picked = [sb(f"picked{h}", [P, J], F32) for h in range(HALVES)]
 
-        def pick(h, j0, n):
-            nc.vector.tensor_copy(picked[h][:, j0 : j0 + n], ds[h][:].indirect(places[:, j0 // 16 : (j0 + n) // 16]))
+        def slope(h, s):
+            nc.vector.scalar_tensor_tensor(
+                ds[h][:, s * SIDE : (s + 1) * SIDE], squares[h, s], 1.0, minus_c0[h, s][:], ALU.subtract, ALU.mult
+            )
 
-        def give(h, j0, n, tag):
-            c = slice(j0, j0 + n)
-            result = sb(f"result{h}{j0}", [P, n], F32, tag=tag)
+        def pick(h, start, count):
+            nc.vector.tensor_copy(
+                picked[h][:, start : start + count], ds[h][:].indirect(entries(places, start, count))
+            )
+
+        def give(h, start, count, tag=None):
+            c = slice(start, start + count)
+            result = sb(f"result{h}_{start}", [P, count], F32, tag=tag)
             nc.vector.scalar_tensor_tensor(
                 result[:], picked[h][:, c], gains[:, h : h + 1], old_sb[:, h, c], ALU.mult, ALU.add
             )
             nc.sync.dma_start(out[h * P : (h + 1) * P, c], result[:])
 
-        put(0, a0[0], 0, HJ)
-        put(0, a0[1], HJ, HJ)
-        put(1, a1, 0, J)
-        quantise_wo()
-        quantise_dy(0, 1)
-        tanh(0)
-        quantise_dy(1, 2)
-        square(0)
-        last_layer(0, 0, 1)
-        last_layer(0, 1, 2)
-        last_layer(1, 0, 1)
-        last_layer(1, 1, 1)
-        add1(0)
-        add1(1)
-        act1(0)
-        act1(1)
-        mult(0, 0)
-        mult(0, 1)
-        mult(1, 0)
+        slope(0, 0)
+        slope(0, 1)
+        slope(1, 0)
         pick(0, 0, J)
-        mult(1, 1)
-        give(0, 0, J, "u210")
-        pick(1, 0, HJ)
-        pick(1, HJ, HJ)
-        give(1, 0, HJ, None)
-        give(1, HJ, HJ, None)
+        slope(1, 1)
+        give(0, 0, J, tag="squares1_0")
+        for start in range(0, J, PIECE):
+            pick(1, start, PIECE)
+        for start in range(0, J, PIECE):
+            give(1, start, PIECE)

from contextlib import ExitStack

import concourse.mybir as mybir
from concourse.masks import make_identity

K, R, F, T, J, U = 512, 256, 512, 2048, 512, 1024
FLOPS = 2 * K * R * J + 2 * F * R * U

F32 = mybir.dt.float32
BF16 = mybir.dt.bfloat16
I32 = mybir.dt.int32
U32 = mybir.dt.uint32
U16 = mybir.dt.uint16
U8 = mybir.dt.uint8
FP8X4 = mybir.dt.float8_e4m3fn_x4
ACT = mybir.ActivationFunctionType
ALU = mybir.AluOpType

P = 128
PACK = 4
SIDE = 512
PER_COL = 16
HALVES = R // P
SIDES = U // SIDE
RUN = 4
PIECE = 256


def interleave_views(dst, src):
    return (
        dst.rearrange("p (c i) t -> p c t i", i=RUN),
        src.rearrange("p t (c i) -> p c t i", i=RUN),
    )


def tile_attend_cpageput_kernel(tc, tab_words, tab_scales, w1, gain, ground, wo, dy, old, offs, offs2, out):
    nc = tc.nc
    with ExitStack() as ctx:
        keep = ctx.enter_context(tc.tile_pool(name="keep", bufs=1))
        psum = ctx.enter_context(tc.psum_pool(name="psum", bufs=1))

        def sb(name, shape, dtype, tag=None):
            return keep.tile(shape, dtype, name=name, tag=tag or name, align_bytes=64)

        def bank(tag, name):
            return psum.tile([P, SIDE], F32, name=name, tag=tag)

        def entries(lists, start, count):
            return lists[:, start // PER_COL : (start + count) // PER_COL]

        def quantise(codes, scales, woven):
            nc.vector.quantize_mx(codes.bitcast(FP8X4), scales, woven.rearrange("p c t -> p (c t)"))

        def product(acc, h, w_codes, w_scales, x_codes, x_scales):
            rows = slice(h * P, (h + 1) * P)
            nc.tensor.matmul_mx(
                acc,
                lhsT=w_codes[:, rows].bitcast(FP8X4),
                lhsT_scale=w_scales[:, rows],
                rhs=x_codes.bitcast(FP8X4),
                rhs_scale=x_scales,
                start=True,
                stop=True,
            )

        cols = keep.tile([P, J // PER_COL], U16, name="cols")
        places = keep.tile([P, J // PER_COL], U16, name="places")
        words = sb("words", [P, T], U32)
        scale_bytes = sb("scale_bytes", [P, T], U8)
        gains = sb("gains", [P, HALVES], F32)
        gain_rows = sb("gain_rows", [P, P], F32)
        w1_raw = sb("w1_raw", [P, PACK, R], F32)
        wo_raw = sb("wo_raw", [P, PACK, R], F32)
        dy_side0 = sb("dy_side0", [P, PACK, SIDE], F32)
        dy_side1 = [sb(f"dy_side1_{i}", [P, PACK, PIECE], F32) for i in range(SIDE // PIECE)]
        ground0 = sb("ground0", [P, U], F32)
        ground1 = [sb(f"ground1_{s}", [P, SIDE], F32) for s in range(SIDES)]
        old_sb = sb("old_sb", [P, HALVES, J], F32)
        page = [sb(f"page{h}", [P, U], F32) for h in range(HALVES)]
        ident = sb("ident", [P, P], F32)

        nc.vector.memset(scale_bytes[:].bitcast(I32), 0)
        nc.vector.memset(gain_rows[:], 0.0)
        dy_rows = dy.rearrange("(p t) u -> p t u", t=PACK)
        nc.sync.dma_start(cols[:], offs)
        nc.sync.dma_start(w1_raw[:], w1.rearrange("(p t) r -> p t r", t=PACK))
        for q in range(4):
            nc.sync.dma_start(
                scale_bytes[32 * q : 32 * q + 4, :].bitcast(I32), tab_scales[0, 4 * q : 4 * q + 4, :].bitcast(I32)
            )
        nc.sync.dma_start(gain_rows[0:HALVES, :], gain.rearrange("(h p) o -> h (p o)", p=P))
        nc.sync.dma_start(words[:].bitcast(I32), tab_words[0].rearrange("p n t -> p (n t)").bitcast(I32))
        nc.sync.dma_start(wo_raw[:], wo.rearrange("(p t) r -> p t r", t=PACK))
        nc.sync.dma_start(places[:], offs2)
        nc.sync.dma_start(dy_side0[:], dy_rows[:, :, 0:SIDE])
        nc.sync.dma_start(ground0[:], ground[0:P, :])
        for i, raw in enumerate(dy_side1):
            nc.sync.dma_start(raw[:], dy_rows[:, :, SIDE + i * PIECE : SIDE + (i + 1) * PIECE])
        nc.sync.dma_start(ground1[0][:], ground[P:R, 0:SIDE])
        nc.sync.dma_start(old_sb[:], old.rearrange("(h p) j -> p h j", p=P))
        nc.sync.dma_start(ground1[1][:], ground[P:R, SIDE:U])

        for h in range(HALVES):
            nc.vector.memset(page[h][:], 0.0)
        make_identity(nc, ident[:])

        gain_bank = bank("gain", "gain_bank")
        nc.tensor.transpose(gain_bank[:, 0:P], gain_rows[:], ident[:])
        nc.scalar.copy(gains[:], gain_bank[:, 0:HALVES])

        got_words = sb("got_words", [P, J], U32)
        got_bytes = sb("got_bytes", [P, J], U8)
        w1_bf = sb("w1_bf", [P, R, PACK], BF16)
        w1_codes = sb("w1_codes", [P, R], U32)
        w1_scales = sb("w1_scales", [P, R], U8)
        nc.vector.tensor_copy(got_bytes[:], scale_bytes[:].indirect(cols[:]))

        nc.vector.tensor_copy(*interleave_views(w1_bf[:, 0:P, :], w1_raw[:, :, 0:P]))
        quantise(w1_codes[:, 0:P], w1_scales[:, 0:P], w1_bf[:, 0:P, :])
        nc.scalar.activation(*interleave_views(w1_bf[:, P:R, :], w1_raw[:, :, P:R]), ACT.Copy)
        quantise(w1_codes[:, P:R], w1_scales[:, P:R], w1_bf[:, P:R, :])

        a0 = [bank(f"upright{i}", f"a0_{i}") for i in range(J // PIECE)]
        a1 = bank("a1", "a1")
        for i, acc in enumerate(a0):
            c = slice(i * PIECE, (i + 1) * PIECE)
            nc.vector.tensor_copy(got_words[:, c], words[:].indirect(entries(cols, i * PIECE, PIECE)))
            product(acc[:, 0:PIECE], 0, w1_codes, w1_scales, got_words[:, c], got_bytes[:, c])
        product(a1[:], 1, w1_codes, w1_scales, got_words[:], got_bytes[:])

        def put(h, acc, start, count):
            h1 = sb(f"h1_{h}_{start}", [P, count], F32)
            nc.scalar.activation(h1[:], acc[:, 0:count], ACT.Copy, scale=gains[:, h : h + 1])
            nc.vector.tensor_copy(page[h][:].indirect(entries(places, start, count)), h1[:])

        for i, acc in enumerate(a0):
            put(0, acc, i * PIECE, PIECE)
        put(1, a1, 0, J)

        wo_bf = sb("wo_bf", [P, R, PACK], BF16)
        wo_codes = sb("wo_codes", [P, R], U32)
        wo_scales = sb("wo_scales", [P, R], U8)
        dy_bf = [sb(f"dy_bf{s}", [P, SIDE, PACK], BF16) for s in range(SIDES)]
        dy_codes = [sb(f"dy_codes{s}", [P, SIDE], U32) for s in range(SIDES)]
        dy_scales = [sb(f"dy_scales{s}", [P, SIDE], U8) for s in range(SIDES)]

        nc.vector.tensor_scalar(*interleave_views(wo_bf[:], wo_raw[:]), -1.0, None, ALU.mult)
        quantise(wo_codes[:], wo_scales[:], wo_bf[:])

        def quantise_dy(s, c, raw):
            nc.scalar.activation(*interleave_views(dy_bf[s][:, c, :], raw[:]), ACT.Copy)
            quantise(dy_codes[s][:, c], dy_scales[s][:, c], dy_bf[s][:, c, :])

        quantise_dy(0, slice(0, SIDE), dy_side0)

        turned = [bank(f"turned{s}", f"sum0_{s}") for s in range(SIDES)]
        blocks = SIDE // P
        for source, opens in ((ground0, True), (page[0], False)):
            for s in range(SIDES):
                for b in range(blocks):
                    nc.tensor.matmul(
                        turned[s][:, b * P : (b + 1) * P],
                        source[:, s * SIDE + b * P : s * SIDE + (b + 1) * P],
                        ident[:],
                        start=(opens and b == 0),
                        stop=(not opens and b == blocks - 1),
                        is_transpose=True,
                    )
        tanh0_turned = [sb(f"tanh0_turned{s}", [P, SIDE], F32) for s in range(SIDES)]
        for s in range(SIDES):
            nc.scalar.activation(tanh0_turned[s][:], turned[s][:], ACT.Tanh)

        for i, raw in enumerate(dy_side1):
            quantise_dy(1, slice(i * PIECE, (i + 1) * PIECE), raw)

        squares0 = sb("squares0", [P, U], F32)
        squares = {(0, s): squares0[:, s * SIDE : (s + 1) * SIDE] for s in range(SIDES)}
        for s in range(SIDES):
            upright = bank(f"upright{s}", f"tanh0_{s}")
            for b in range(blocks):
                nc.tensor.transpose(
                    upright[:, b * P : (b + 1) * P], tanh0_turned[s][:, b * P : (b + 1) * P], ident[:]
                )
            nc.scalar.activation(squares[0, s], upright[:], ACT.Square)

        minus_c0 = {}
        for h in range(HALVES):
            for s in range(SIDES):
                minus_c0[h, s] = bank(f"turned{1 - s}" if h == 0 else f"upright{s}", f"minus_c0_{h}{s}")
                product(minus_c0[h, s][:], h, wo_codes, wo_scales, dy_codes[s][:], dy_scales[s][:])

        sum1 = sb("sum1", [P, U], F32)
        for s in range(SIDES):
            c = slice(s * SIDE, (s + 1) * SIDE)
            nc.vector.tensor_tensor(sum1[:, c], page[1][:, c], ground1[s][:], ALU.add)
        for s in range(SIDES):
            tanh1 = sb(f"tanh1_{s}", [P, SIDE], F32)
            nc.scalar.activation(tanh1[:], sum1[:, s * SIDE : (s + 1) * SIDE], ACT.Tanh)
            squares[1, s] = sb(f"squares1_{s}", [P, SIDE], F32)[:]
            nc.scalar.activation(squares[1, s], tanh1[:], ACT.Square)

        ds = [sb(f"ds{h}", [P, U], F32) for h in range(HALVES)]
        picked = [sb(f"picked{h}", [P, J], F32) for h in range(HALVES)]

        def slope(h, s):
            nc.vector.scalar_tensor_tensor(
                ds[h][:, s * SIDE : (s + 1) * SIDE], squares[h, s], 1.0, minus_c0[h, s][:], ALU.subtract, ALU.mult
            )

        def pick(h, start, count):
            nc.vector.tensor_copy(
                picked[h][:, start : start + count], ds[h][:].indirect(entries(places, start, count))
            )

        def give(h, start, count, tag=None):
            c = slice(start, start + count)
            result = sb(f"result{h}_{start}", [P, count], F32, tag=tag)
            nc.vector.scalar_tensor_tensor(
                result[:], picked[h][:, c], gains[:, h : h + 1], old_sb[:, h, c], ALU.mult, ALU.add
            )
            nc.sync.dma_start(out[h * P : (h + 1) * P, c], result[:])

        slope(0, 0)
        slope(0, 1)
        slope(1, 0)
        pick(0, 0, J)
        slope(1, 1)
        give(0, 0, J, tag="squares1_0")
        for start in range(0, J, PIECE):
            pick(1, start, PIECE)
        for start in range(0, J, PIECE):
            give(1, start, PIECE)
